import numpy as np
import ml_dtypes


def mxq(x, axis, fmt="e4m3"):
    dtype, down = {"e4m3": (ml_dtypes.float8_e4m3fn, 7), "e5m2": (ml_dtypes.float8_e5m2, 14)}[fmt]
    v = np.moveaxis(np.asarray(x, np.float32).astype(ml_dtypes.bfloat16).astype(np.float64), axis, -1)
    blocks = v.reshape(v.shape[:-1] + (-1, 32))
    amax = np.abs(blocks).max(-1, keepdims=True)
    byte = np.maximum(np.where(amax > 0, np.frexp(amax)[1] - 1 + 127, 0) - down, 1)
    scale = np.exp2(byte - 127.0)
    codes = (blocks / scale).astype(np.float32).astype(dtype).astype(np.float64)
    return np.moveaxis((codes * scale).reshape(v.shape), -1, axis)


WIDE = False


def mx_kscale(k):
    if not WIDE:
        return np.ones(k)
    levels = np.array([10, -10, 5, -5, 0])
    if k % 512:
        return np.exp2(np.random.permutation(np.resize(levels, k // 32))).repeat(32)
    a = np.empty((k // 512, 16))
    for p in range(k // 512):
        a[p, :8] = np.random.permutation(np.resize(levels, 8))
        for g in range(8):
            far = levels[np.abs(levels - a[p, g]) >= 10]
            a[p, g + 8] = far[np.random.randint(len(far))]
    return np.exp2(a.ravel()).repeat(32)


def f64(x):
    return np.asarray(x).astype(np.float64)


def striped(idx):
    return np.tile(idx.reshape(-1, 16).T, (8, 1)).astype(np.uint16)


def unstriped(offs):
    return offs[:16].T.reshape(-1).astype(np.int64)


E2M1 = np.array([0.0, 0.5, 1.0, 1.5, 2.0, 3.0, 4.0, 6.0, -0.0, -0.5, -1.0, -1.5, -2.0, -3.0, -4.0, -6.0])


def pack_weight(w, fmt):
    k, n = w.shape
    w = f64(np.asarray(w, np.float32).astype(ml_dtypes.bfloat16)).reshape(k // 32, 32, n)
    amax = np.abs(w).max(1)
    if fmt == "e4m3":
        byte = np.frexp(amax)[1] - 1 + 127 - 7
    else:
        mant, ex = np.frexp(amax / 6.0)
        byte = np.where(mant > 0.5, ex, ex - 1) + 127
    byte = np.clip(np.where(amax > 0, byte, 1), 1, 254)
    scaled = (w * np.exp2(127.0 - byte)[:, None, :]).reshape(k, n).astype(np.float32)
    by_word = np.ascontiguousarray(scaled.reshape(k // 512, 128, 4, n).transpose(0, 1, 3, 2))
    if fmt == "e4m3":
        words = by_word.astype(ml_dtypes.float8_e4m3fn).view(np.uint8)
    else:
        c = by_word.astype(ml_dtypes.float4_e2m1fn).view(np.uint8) & 0xF
        words = (c[..., 0::2] | (c[..., 1::2] << 4)).reshape(k // 512, 128, 2 * n)
    return np.ascontiguousarray(words), np.ascontiguousarray(byte.astype(np.uint8).reshape(k // 512, 16, n))


def unpack_weight(words, scales, fmt):
    g, _, n = scales.shape
    words = np.ascontiguousarray(words).reshape(g, 128, n, -1)
    if fmt == "e4m3":
        vals = words.view(ml_dtypes.float8_e4m3fn).astype(np.float64)
    else:
        nib = np.empty((g, 128, n, 4), np.uint8)
        nib[..., 0::2] = words & 0xF
        nib[..., 1::2] = words >> 4
        vals = E2M1[nib]
    vals = vals * np.repeat(np.exp2(scales.astype(np.float64) - 127.0), 8, axis=1)[..., None]
    return vals.transpose(0, 1, 3, 2).reshape(g * 512, n)


def silu(v):
    return v / (1.0 + np.exp(-np.maximum(v, -700.0)))


K, T, E, C, N = 512, 512, 12, 128, 256
TOP = 3


def by_expert(wq, xq):
    return np.concatenate([wq[e].T @ xq[:, e * C:(e + 1) * C] for e in range(E)], axis=1)


def setup_inputs():
    n = np.random.standard_normal
    s = mx_kscale(K)[:, None]
    deal = np.repeat(np.arange(E), C).reshape(TOP, T)[:, np.random.permutation(T)]
    deal = np.take_along_axis(deal, np.argsort(np.random.rand(TOP, T), axis=0), axis=0)
    for _ in range(8):
        s_, t_ = np.random.permutation(T).reshape(2, -1); r = np.random.randint(TOP, size=T // 2); x, y = deal[r, s_].copy(), deal[r, t_].copy()
        ok = ~((deal[:, s_] == y).any(0) | (deal[:, t_] == x).any(0)); deal[r[ok], s_[ok]] = y[ok]; deal[r[ok], t_[ok]] = x[ok]
    order = np.lexsort((np.random.rand(TOP * T), deal.reshape(-1)))
    slot_token = order % T; pos = np.empty(TOP * T, np.int64); pos[order] = np.arange(TOP * T); pos = pos.reshape(TOP, T)
    g = np.random.uniform(0.5, 1.5, (TOP, T)); g = g / g.sum(0)
    x = pack_weight(n((K, T)) * s, "e4m3")
    return {
        "x_words": x[0],
        "x_scales": x[1],
        "w": (n((E + 1, K, N)) / np.sqrt(K) / s[None]).astype(np.float32),
        "b": (0.3 * n((N, E + 1))).astype(np.float32),
        "gate": np.stack([np.tile(r, (N, 1)) for r in g]).astype(np.float32),
        "offs": striped(slot_token),
        "pos1": striped(pos[0]),
        "pos2": striped(pos[1]),
        "pos3": striped(pos[2]),
    }


def reference(x_words, x_scales, w, b, gate, offs, pos1, pos2, pos3):
    idx = unstriped(offs)
    wq = mxq(f64(w), 1, "e4m3")
    xs = unpack_weight(x_words, x_scales, "e4m3")
    ys = silu((wq[E].T @ xs) + f64(b)[:, E:])
    xq = unpack_weight(x_words, x_scales, "e4m3")[:, idx]
    y = by_expert(wq, xq)
    y = silu(y + np.repeat(f64(b)[:, :E], C, axis=1))
    return ys + sum(f64(gate[r]) * y[:, unstriped(p)] for r, p in enumerate((pos1, pos2, pos3)))

@@ -1,0 +1,164 @@
+from contextlib import ExitStack
+
+import concourse.mybir as mybir
+from concourse.masks import make_identity
+
+K, T, E, C, N = 512, 512, 12, 128, 256
+TOP = 3
+SLOTS = E * C
+FLOPS = 2 * K * N * (SLOTS + T)
+
+F32 = mybir.dt.float32
+BF16 = mybir.dt.bfloat16
+I32 = mybir.dt.int32
+U32 = mybir.dt.uint32
+U16 = mybir.dt.uint16
+U8 = mybir.dt.uint8
+FP8X4 = mybir.dt.float8_e4m3fn_x4
+SILU = mybir.ActivationFunctionType.Silu
+MULT = mybir.AluOpType.mult
+ADD = mybir.AluOpType.add
+
+P = 128
+PACK = 4
+HALVES = N // P
+GATHER_EXPERTS = 3
+CASTS = {
+    6: (("vector", 0, N, "grouped3"),),
+    7: (("vector", 0, N, "grouped4"),),
+    8: (("scalar", 0, N, "grouped3"),),
+    9: (("vector", 0, N, "grouped4"),),
+    10: (("vector", 0, P, "grouped3"), ("scalar", P, N, "codes8")),
+    11: (("vector", 0, P, "codes9"), ("scalar", P, N, "bias0")),
+    12: (("scalar", 0, N, "raw11"),),
+}
+
+
+def tile_moe_shr_lin_silu_kernel(tc, x_words, x_scales, w, b, gate, offs, pos1, pos2, pos3, out):
+    nc = tc.nc
+    with ExitStack() as ctx:
+        keep = ctx.enter_context(tc.tile_pool(name="keep", bufs=1))
+        psum = ctx.enter_context(tc.psum_pool(name="psum", bufs=2))
+        psum_mx = ctx.enter_context(tc.psum_pool(name="psum_mx", bufs=4))
+
+        offs_sb = keep.tile([P, SLOTS // 16], U16, name="offs_sb")
+        pos_sb = [keep.tile([P, T // 16], U16, name="pos_sb%d" % r) for r in range(TOP)]
+        x_sb = keep.tile([P, T], I32, name="x_sb", align_bytes=64)
+        xs_sb = keep.tile([P, T], U8, name="xs_sb", align_bytes=64)
+        b_sb = keep.tile([P, HALVES, 16], F32, name="b_sb")
+        bias0 = keep.tile([P, E], F32, name="bias0", align_bytes=64)
+        raw = [keep.tile([P, PACK, N], F32, name="raw%d" % e, align_bytes=64) for e in range(E + 1)]
+        gate_sb = [[keep.tile([P, T], F32, name="gate%d_%d" % (h, r)) for r in range(TOP)] for h in range(HALVES)]
+        warm = keep.tile([P, 8], F32, name="warm")
+        ident = keep.tile([P, P], F32, name="ident")
+
+        nc.vector.memset(xs_sb[:].bitcast(I32), 0)
+        nc.vector.memset(warm[:, 0:1], 0.0)
+        nc.scalar.activation(out=warm[:, 4:5], in_=warm[:, 0:1], func=SILU)
+
+        def load_w(e):
+            nc.sync.dma_start(out=raw[e][:], in_=w[e].rearrange("(p j) n -> p j n", j=PACK))
+
+        def load_gate(h, r):
+            nc.sync.dma_start(out=gate_sb[h][r][:], in_=gate[r, h * P:(h + 1) * P, :])
+
+        nc.sync.dma_start(offs_sb[:], offs)
+        nc.sync.dma_start(out=x_sb[:], in_=x_words[0].rearrange("p t r -> p (t r)").bitcast(I32))
+        for q in range(4):
+            nc.sync.dma_start(out=xs_sb[32 * q:32 * q + 4, :].bitcast(I32), in_=x_scales[0, 4 * q:4 * q + 4, :].bitcast(I32))
+        nc.scalar.dma_start(out=b_sb[:, :, 0:E + 1], in_=b.rearrange("(h p) e -> p h e", p=P))
+        nc.gpsimd.tensor_copy(out=bias0[:], in_=b_sb[:, 0, 0:E])
+        make_identity(nc, ident[:])
+        for e in range(E):
+            load_w(e)
+            if e == 6:
+                for tile_r, pos in zip(pos_sb, (pos1, pos2, pos3)):
+                    nc.sync.dma_start(tile_r[:], pos)
+        load_gate(0, 0)
+        load_gate(0, 1)
+        load_w(E)
+        load_gate(0, 2)
+        for r in range(TOP):
+            load_gate(1, r)
+
+        y = [keep.tile([P, SLOTS], F32, name="y%d" % h) for h in range(HALVES)]
+        ys = [keep.tile([P, T], F32, name="ys%d" % h) for h in range(HALVES)]
+        width = GATHER_EXPERTS * C
+        xg = [keep.tile([P, width], U32, name="xg%d" % g, align_bytes=64) for g in range(E // GATHER_EXPERTS)]
+        xsg = [keep.tile([P, width], U8, name="xsg%d" % g, align_bytes=64) for g in range(E // GATHER_EXPERTS)]
+
+        def gather_tokens(g):
+            lst = offs_sb[:, g * width // 16:(g + 1) * width // 16]
+            nc.vector.tensor_copy(out=xg[g][:], in_=x_sb[:].bitcast(U32).indirect(lst))
+            nc.vector.tensor_copy(out=xsg[g][:], in_=xs_sb[:].indirect(lst))
+
+        def expert(e):
+            codes = keep.tile([P, N], U32, name="codes%d" % e, align_bytes=64)
+            scales = keep.tile([P, N], U8, name="scales%d" % e, align_bytes=64)
+            for engine, c0, c1, tag in CASTS.get(e, (("scalar", 0, N, "grouped%d" % e),)):
+                copy = nc.vector.tensor_copy if engine == "vector" else nc.scalar.copy
+                grouped = keep.tile([P, c1 - c0, PACK], BF16, name="grouped%d_%d" % (e, c0), tag=tag, align_bytes=64)
+                copy(out=grouped[:].rearrange("p (c i) t -> p c t i", i=2),
+                     in_=raw[e][:, :, c0:c1].rearrange("p t (c i) -> p c t i", i=2))
+                nc.vector.quantize_mx(out=codes[:, c0:c1].bitcast(FP8X4), scales=scales[:, c0:c1],
+                                      in_=grouped[:].rearrange("p n t -> p (n t)"))
+
+            for h in range(HALVES):
+                cols = slice(h * P, (h + 1) * P)
+                if e < E:
+                    g, c0 = divmod(e, GATHER_EXPERTS)
+                    slots = slice(c0 * C, (c0 + 1) * C)
+                    words, word_scales, dst = xg[g][:, slots], xsg[g][:, slots], y[h][:, e * C:(e + 1) * C]
+                else:
+                    words, word_scales, dst = x_sb[:], xs_sb[:], ys[h][:]
+                acc = psum_mx.tile([P, words.shape[1]], F32, name="acc")
+                nc.tensor.matmul_mx(out=acc[:], lhsT=codes[:, cols].bitcast(FP8X4), lhsT_scale=scales[:, cols],
+                                    rhs=words.bitcast(FP8X4), rhs_scale=word_scales, start=True, stop=True)
+                nc.scalar.activation(out=dst, in_=acc[:], func=SILU,
+                                     bias=bias0[:, e:e + 1] if h == 0 and e < E else b_sb[:, h, e:e + 1])
+
+        for e in range(E + 1):
+            if e < E and e % GATHER_EXPERTS == 0:
+                gather_tokens(e // GATHER_EXPERTS)
+            expert(e)
+
+        def products(h, t0, t1, tags):
+            prods = []
+            for r in range(TOP):
+                prod = keep.tile([P, t1 - t0], F32, name="prod%d_%d_%d" % (h, t0, r), tag=tags[r], align_bytes=64)
+                nc.vector.tensor_tensor(out=prod[:], in0=y[h][:].indirect(pos_sb[r][:, t0 // 16:t1 // 16]),
+                                        in1=gate_sb[h][r][:, t0:t1], op=MULT)
+                prods.append(prod)
+            return prods
+
+        def sum_on_tensor(h, t0, t1, tags):
+            prods = products(h, t0, t1, tags)
+            terms = [prods[0][:], prods[1][:], ys[h][:, t0:t1], prods[2][:]]
+            blocks = [slice(j, j + P) for j in range(0, t1 - t0, P)]
+            turned = psum.tile([P, t1 - t0], F32, name="turned")
+            for i, term in enumerate(terms):
+                for j, blk in enumerate(blocks):
+                    nc.tensor.matmul(out=turned[:, blk], lhsT=term[:, blk], rhs=ident[:], is_transpose=True,
+                                     start=(i == 0 and j == 0), stop=(i == len(terms) - 1 and j == len(blocks) - 1))
+            turned_sb = keep.tile([P, t1 - t0], F32, name="turned_sb%d_%d" % (h, t0))
+            nc.scalar.copy(out=turned_sb[:], in_=turned[:])
+            back = psum.tile([P, t1 - t0], F32, name="back")
+            for blk in blocks:
+                nc.tensor.transpose(back[:, blk], turned_sb[:, blk], ident[:])
+            res = keep.tile([P, t1 - t0], F32, name="res%d_%d" % (h, t0))
+            nc.scalar.copy(out=res[:], in_=back[:])
+            nc.sync.dma_start(out=out[h * P:(h + 1) * P, t0:t1], in_=res[:])
+
+        def sum_on_vector(h, t0, t1, tags):
+            prods = products(h, t0, t1, tags)
+            s1 = keep.tile([P, t1 - t0], F32, name="s1")
+            s2 = keep.tile([P, t1 - t0], F32, name="s2")
+            res = keep.tile([P, t1 - t0], F32, name="res_last")
+            nc.vector.tensor_tensor(out=s1[:], in0=ys[h][:, t0:t1], in1=prods[0][:], op=ADD)
+            nc.vector.tensor_tensor(out=s2[:], in0=prods[1][:], in1=prods[2][:], op=ADD)
+            nc.vector.tensor_tensor(out=res[:], in0=s1[:], in1=s2[:], op=ADD)
+            nc.sync.dma_start(out=out[h * P:(h + 1) * P, t0:t1], in_=res[:])
+
+        sum_on_tensor(0, 0, T, ("prod0", "prod1", "bias0"))
+        sum_on_tensor(1, 0, T // 2, ("raw11", "codes12", "scales12"))
+        sum_on_vector(1, T // 2, T, ("bias0", "raw11", "codes12"))

@@ -23,142 +23,182 @@ P = 128
 PACK = 4
 HALVES = N // P
 GATHER_EXPERTS = 3
-CASTS = {
-    6: (("vector", 0, N, "grouped3"),),
-    7: (("vector", 0, N, "grouped4"),),
-    8: (("scalar", 0, N, "grouped3"),),
-    9: (("vector", 0, N, "grouped4"),),
-    10: (("vector", 0, P, "grouped3"), ("scalar", P, N, "codes8")),
-    11: (("vector", 0, P, "codes9"), ("scalar", P, N, "bias0")),
-    12: (("scalar", 0, N, "raw11"),),
-}
+RUN = 2
+LOADS = ["offs","xw","w0","w1","xs","w2","w3","w4","w5","w6","w7","b","w8","w9","w10","w11","pos0","pos1","w12","g00","g01","pos2","g02","gBl","gBr"]
+SPLIT = []
+CASTS = ["S","S","S","S","S","S","S","VV","VV","VV","VV","VV","VV"]
+TAGS = {}
+BANKS = []
+TERMS = ["s123","s123"]
+PIECES = [["A",0,0,512,"pe"],["Bl",1,0,256,"pe"],["Br",1,256,512,"v"]]
+BIAS_COPIES = []
 
 
 def tile_moe_shr_lin_silu_kernel(tc, x_words, x_scales, w, b, gate, offs, pos1, pos2, pos3, out):
     nc = tc.nc
     with ExitStack() as ctx:
         keep = ctx.enter_context(tc.tile_pool(name="keep", bufs=1))
-        psum = ctx.enter_context(tc.psum_pool(name="psum", bufs=2))
+        psum = ctx.enter_context(tc.psum_pool(name="psum", bufs=1))
         psum_mx = ctx.enter_context(tc.psum_pool(name="psum_mx", bufs=4))
 
-        offs_sb = keep.tile([P, SLOTS // 16], U16, name="offs_sb")
-        pos_sb = [keep.tile([P, T // 16], U16, name="pos_sb%d" % r) for r in range(TOP)]
-        x_sb = keep.tile([P, T], I32, name="x_sb", align_bytes=64)
-        xs_sb = keep.tile([P, T], U8, name="xs_sb", align_bytes=64)
-        b_sb = keep.tile([P, HALVES, 16], F32, name="b_sb")
-        bias0 = keep.tile([P, E], F32, name="bias0", align_bytes=64)
-        raw = [keep.tile([P, PACK, N], F32, name="raw%d" % e, align_bytes=64) for e in range(E + 1)]
-        gate_sb = [[keep.tile([P, T], F32, name="gate%d_%d" % (h, r)) for r in range(TOP)] for h in range(HALVES)]
-        warm = keep.tile([P, 8], F32, name="warm")
-        ident = keep.tile([P, P], F32, name="ident")
+        def new(name, shape, dtype):
+            return keep.tile(shape, dtype, name=name, tag=TAGS.get(name, name), align_bytes=64)
 
-        nc.vector.memset(xs_sb[:].bitcast(I32), 0)
-        nc.vector.memset(warm[:, 0:1], 0.0)
-        nc.scalar.activation(out=warm[:, 4:5], in_=warm[:, 0:1], func=SILU)
+        offs_sb = new("offs", [P, SLOTS // 16], U16)
+        pos_sb = [new("pos%d" % r, [P, T // 16], U16) for r in range(TOP)]
+        x_sb = new("xw", [P, T], I32)
+        xs_sb = new("xs", [P, T], U8)
+        b_sb = new("b", [P, HALVES, 16], F32)
+        gate_sb = {}
+        for name, h, t0, t1, how in PIECES:
+            if "g" + name in LOADS:
+                whole = new("g" + name, [P, TOP, t1 - t0], F32)
+                gate_sb[name] = [whole[:, r, :] for r in range(TOP)]
+                gate_sb["g" + name] = (whole, h, t0, t1)
+            else:
+                gate_sb[name] = [new("g%d%d" % (h, r), [P, T], F32)[:] for r in range(TOP)]
+        warm = new("warm", [P, 32], F32)
+        ident = new("ident", [P, P], F32)
+        raw = {}
+        for e in range(E + 1):
+            if e in SPLIT:
+                raw["%dA" % e] = new("raw%dA" % e, [P, PACK, P], F32)
+                raw["%dB" % e] = new("raw%dB" % e, [P, PACK, P], F32)
+            else:
+                raw["%d" % e] = new("raw%d" % e, [P, PACK, N], F32)
 
-        def load_w(e):
-            nc.sync.dma_start(out=raw[e][:], in_=w[e].rearrange("(p j) n -> p j n", j=PACK))
+        nc.gpsimd.memset(xs_sb[:].bitcast(I32), 0)
+        nc.gpsimd.memset(warm[:, 0:1], 0.0)
+        nc.scalar.activation(out=warm[:, 16:17], in_=warm[:, 0:1], func=SILU)
 
-        def load_gate(h, r):
-            nc.sync.dma_start(out=gate_sb[h][r][:], in_=gate[r, h * P:(h + 1) * P, :])
+        for name in LOADS:
+            if name == "offs":
+                nc.sync.dma_start(offs_sb[:], offs)
+            elif name == "xw":
+                nc.sync.dma_start(out=x_sb[:], in_=x_words[0].rearrange("p t r -> p (t r)").bitcast(I32))
+            elif name == "xs":
+                for q in range(4):
+                    nc.sync.dma_start(out=xs_sb[32 * q:32 * q + 4, :].bitcast(I32), in_=x_scales[0, 4 * q:4 * q + 4, :].bitcast(I32))
+            elif name == "b":
+                nc.sync.dma_start(out=b_sb[:, :, 0:E + 1], in_=b.rearrange("(h p) e -> p h e", p=P))
+            elif name.startswith("pos"):
+                r = int(name[3])
+                nc.sync.dma_start(pos_sb[r][:], (pos1, pos2, pos3)[r])
+            elif name in gate_sb:
+                whole, h, t0, t1 = gate_sb[name]
+                nc.sync.dma_start(out=whole[:], in_=gate[:, h * P:(h + 1) * P, t0:t1].rearrange("r p t -> p r t"))
+            elif name.startswith("g"):
+                nc.sync.dma_start(out=gate_sb["A"][int(name[2])], in_=gate[int(name[2]), 0:P, :])
+            elif name[-1] in "AB":
+                h = "AB".index(name[-1])
+                nc.sync.dma_start(out=raw[name[1:]][:], in_=w[int(name[1:-1])].rearrange("(p j) n -> p j n", j=PACK)[:, :, h * P:(h + 1) * P])
+            else:
+                nc.sync.dma_start(out=raw[name[1:]][:], in_=w[int(name[1:])].rearrange("(p j) n -> p j n", j=PACK))
 
-        nc.sync.dma_start(offs_sb[:], offs)
-        nc.sync.dma_start(out=x_sb[:], in_=x_words[0].rearrange("p t r -> p (t r)").bitcast(I32))
-        for q in range(4):
-            nc.sync.dma_start(out=xs_sb[32 * q:32 * q + 4, :].bitcast(I32), in_=x_scales[0, 4 * q:4 * q + 4, :].bitcast(I32))
-        nc.scalar.dma_start(out=b_sb[:, :, 0:E + 1], in_=b.rearrange("(h p) e -> p h e", p=P))
-        nc.gpsimd.tensor_copy(out=bias0[:], in_=b_sb[:, 0, 0:E])
+        bias = [b_sb[:, h, :] for h in range(HALVES)]
+        for h in BIAS_COPIES:
+            own = new("bias%d" % h, [P, 16], F32)
+            nc.gpsimd.tensor_copy(out=own[:, 0:E], in_=b_sb[:, h, 0:E])
+            bias[h] = own[:]
         make_identity(nc, ident[:])
-        for e in range(E):
-            load_w(e)
-            if e == 6:
-                for tile_r, pos in zip(pos_sb, (pos1, pos2, pos3)):
-                    nc.sync.dma_start(tile_r[:], pos)
-        load_gate(0, 0)
-        load_gate(0, 1)
-        load_w(E)
-        load_gate(0, 2)
-        for r in range(TOP):
-            load_gate(1, r)
 
-        y = [keep.tile([P, SLOTS], F32, name="y%d" % h) for h in range(HALVES)]
-        ys = [keep.tile([P, T], F32, name="ys%d" % h) for h in range(HALVES)]
+        y = [new("y%d" % h, [P, SLOTS], F32) for h in range(HALVES)]
+        ys = [new("ys%d" % h, [P, T], F32) for h in range(HALVES)]
         width = GATHER_EXPERTS * C
-        xg = [keep.tile([P, width], U32, name="xg%d" % g, align_bytes=64) for g in range(E // GATHER_EXPERTS)]
-        xsg = [keep.tile([P, width], U8, name="xsg%d" % g, align_bytes=64) for g in range(E // GATHER_EXPERTS)]
+        xg, xsg, banks = {}, {}, {}
 
         def gather_tokens(g):
+            xg[g] = new("xg%d" % g, [P, width], U32)
+            xsg[g] = new("xsg%d" % g, [P, width], U8)
             lst = offs_sb[:, g * width // 16:(g + 1) * width // 16]
             nc.vector.tensor_copy(out=xg[g][:], in_=x_sb[:].bitcast(U32).indirect(lst))
             nc.vector.tensor_copy(out=xsg[g][:], in_=xs_sb[:].indirect(lst))
 
         def expert(e):
-            codes = keep.tile([P, N], U32, name="codes%d" % e, align_bytes=64)
-            scales = keep.tile([P, N], U8, name="scales%d" % e, align_bytes=64)
-            for engine, c0, c1, tag in CASTS.get(e, (("scalar", 0, N, "grouped%d" % e),)):
-                copy = nc.vector.tensor_copy if engine == "vector" else nc.scalar.copy
-                grouped = keep.tile([P, c1 - c0, PACK], BF16, name="grouped%d_%d" % (e, c0), tag=tag, align_bytes=64)
-                copy(out=grouped[:].rearrange("p (c i) t -> p c t i", i=2),
-                     in_=raw[e][:, :, c0:c1].rearrange("p t (c i) -> p c t i", i=2))
-                nc.vector.quantize_mx(out=codes[:, c0:c1].bitcast(FP8X4), scales=scales[:, c0:c1],
+            pieces = CASTS[e]
+            cols = N // len(pieces)
+            operands = []
+            for j, engine in enumerate(pieces):
+                sfx = "" if len(pieces) == 1 else "AB"[j]
+                codes = new("codes%d%s" % (e, sfx), [P, cols], U32)
+                scales = new("scales%d%s" % (e, sfx), [P, cols], U8)
+                grouped = new("grouped%d%s" % (e, sfx), [P, cols, PACK], BF16)
+                src = raw["%d%s" % (e, sfx)][:] if e in SPLIT else raw["%d" % e][:, :, j * cols:(j + 1) * cols]
+                copy = nc.vector.tensor_copy if engine == "V" else nc.scalar.copy
+                copy(out=grouped[:].rearrange("p (c i) t -> p c t i", i=RUN),
+                     in_=src.rearrange("p t (c i) -> p c t i", i=RUN))
+                nc.vector.quantize_mx(out=codes[:].bitcast(FP8X4), scales=scales[:],
                                       in_=grouped[:].rearrange("p n t -> p (n t)"))
+                for c0 in range(0, cols, P):
+                    operands.append((codes[:, c0:c0 + P], scales[:, c0:c0 + P]))
 
             for h in range(HALVES):
-                cols = slice(h * P, (h + 1) * P)
                 if e < E:
                     g, c0 = divmod(e, GATHER_EXPERTS)
                     slots = slice(c0 * C, (c0 + 1) * C)
                     words, word_scales, dst = xg[g][:, slots], xsg[g][:, slots], y[h][:, e * C:(e + 1) * C]
                 else:
                     words, word_scales, dst = x_sb[:], xs_sb[:], ys[h][:]
-                acc = psum_mx.tile([P, words.shape[1]], F32, name="acc")
-                nc.tensor.matmul_mx(out=acc[:], lhsT=codes[:, cols].bitcast(FP8X4), lhsT_scale=scales[:, cols],
+                banked = h == 1 and e < E and len(BANKS) > 0
+                if banked:
+                    k = [i for i in range(len(BANKS)) if e in BANKS[i]][0]
+                    if k not in banks:
+                        banks[k] = psum.tile([P, 4 * C], F32, name="bank%d" % k)
+                    place = BANKS[k].index(e)
+                    acc = banks[k][:, place * C:(place + 1) * C]
+                else:
+                    acc_tile = psum_mx.tile([P, words.shape[1]], F32, name="acc")
+                    acc = acc_tile[:]
+                nc.tensor.matmul_mx(out=acc, lhsT=operands[h][0].bitcast(FP8X4), lhsT_scale=operands[h][1],
                                     rhs=words.bitcast(FP8X4), rhs_scale=word_scales, start=True, stop=True)
-                nc.scalar.activation(out=dst, in_=acc[:], func=SILU,
-                                     bias=bias0[:, e:e + 1] if h == 0 and e < E else b_sb[:, h, e:e + 1])
+                if not banked:
+                    nc.scalar.activation(out=dst, in_=acc, func=SILU, bias=(bias[h] if e < E else b_sb[:, h, :])[:, e:e + 1])
+                elif e == E - 1:
+                    for k in range(len(BANKS)):
+                        for place, e2 in enumerate(BANKS[k]):
+                            nc.scalar.activation(out=y[1][:, e2 * C:(e2 + 1) * C], in_=banks[k][:, place * C:(place + 1) * C],
+                                                 func=SILU, bias=bias[1][:, e2:e2 + 1])
 
         for e in range(E + 1):
             if e < E and e % GATHER_EXPERTS == 0:
                 gather_tokens(e // GATHER_EXPERTS)
             expert(e)
 
-        def products(h, t0, t1, tags):
+        turn_tags = [("tu0", "bk0"), ("bank0", "bank1") if BANKS else ("tu1", "bk1")]
+        on_tensor = 0
+        waiting = []
+        for name, h, t0, t1, how in PIECES:
             prods = []
             for r in range(TOP):
-                prod = keep.tile([P, t1 - t0], F32, name="prod%d_%d_%d" % (h, t0, r), tag=tags[r], align_bytes=64)
+                prod = new("%s%d" % (name, r + 1), [P, t1 - t0], F32)
                 nc.vector.tensor_tensor(out=prod[:], in0=y[h][:].indirect(pos_sb[r][:, t0 // 16:t1 // 16]),
-                                        in1=gate_sb[h][r][:, t0:t1], op=MULT)
+                                        in1=gate_sb[name][r], op=MULT)
                 prods.append(prod)
-            return prods
-
-        def sum_on_tensor(h, t0, t1, tags):
-            prods = products(h, t0, t1, tags)
-            terms = [prods[0][:], prods[1][:], ys[h][:, t0:t1], prods[2][:]]
-            blocks = [slice(j, j + P) for j in range(0, t1 - t0, P)]
-            turned = psum.tile([P, t1 - t0], F32, name="turned")
-            for i, term in enumerate(terms):
-                for j, blk in enumerate(blocks):
-                    nc.tensor.matmul(out=turned[:, blk], lhsT=term[:, blk], rhs=ident[:], is_transpose=True,
-                                     start=(i == 0 and j == 0), stop=(i == len(terms) - 1 and j == len(blocks) - 1))
-            turned_sb = keep.tile([P, t1 - t0], F32, name="turned_sb%d_%d" % (h, t0))
-            nc.scalar.copy(out=turned_sb[:], in_=turned[:])
-            back = psum.tile([P, t1 - t0], F32, name="back")
-            for blk in blocks:
-                nc.tensor.transpose(back[:, blk], turned_sb[:, blk], ident[:])
-            res = keep.tile([P, t1 - t0], F32, name="res%d_%d" % (h, t0))
-            nc.scalar.copy(out=res[:], in_=back[:])
-            nc.sync.dma_start(out=out[h * P:(h + 1) * P, t0:t1], in_=res[:])
-
-        def sum_on_vector(h, t0, t1, tags):
-            prods = products(h, t0, t1, tags)
-            s1 = keep.tile([P, t1 - t0], F32, name="s1")
-            s2 = keep.tile([P, t1 - t0], F32, name="s2")
-            res = keep.tile([P, t1 - t0], F32, name="res_last")
-            nc.vector.tensor_tensor(out=s1[:], in0=ys[h][:, t0:t1], in1=prods[0][:], op=ADD)
-            nc.vector.tensor_tensor(out=s2[:], in0=prods[1][:], in1=prods[2][:], op=ADD)
-            nc.vector.tensor_tensor(out=res[:], in0=s1[:], in1=s2[:], op=ADD)
-            nc.sync.dma_start(out=out[h * P:(h + 1) * P, t0:t1], in_=res[:])
-
-        sum_on_tensor(0, 0, T, ("prod0", "prod1", "bias0"))
-        sum_on_tensor(1, 0, T // 2, ("raw11", "codes12", "scales12"))
-        sum_on_vector(1, T // 2, T, ("bias0", "raw11", "codes12"))
+            res = new("res" + name, [P, t1 - t0], F32)
+            if how == "pe":
+                by_name = {"1": prods[0][:], "2": prods[1][:], "3": prods[2][:], "s": ys[h][:, t0:t1]}
+                terms = [by_name[c] for c in TERMS[on_tensor]]
+                blocks = [slice(j, j + P) for j in range(0, t1 - t0, P)]
+                turned = psum.tile([P, t1 - t0], F32, name="turned" + name, tag=turn_tags[on_tensor][0])
+                for i, term in enumerate(terms):
+                    for j, blk in enumerate(blocks):
+                        nc.tensor.matmul(out=turned[:, blk], lhsT=term[:, blk], rhs=ident[:], is_transpose=True,
+                                         start=(i == 0 and j == 0), stop=(i == len(terms) - 1 and j == len(blocks) - 1))
+                turned_sb = new("ts" + name, [P, t1 - t0], F32)
+                nc.scalar.copy(out=turned_sb[:], in_=turned[:])
+                back = psum.tile([P, t1 - t0], F32, name="back" + name, tag=turn_tags[on_tensor][1])
+                waiting.append((back, turned_sb, blocks, res, h, t0, t1))
+                on_tensor += 1
+                if on_tensor == 2:
+                    for back2, turned2, blocks2, res2, h2, u0, u1 in waiting:
+                        for blk in blocks2:
+                            nc.tensor.transpose(back2[:, blk], turned2[:, blk], ident[:])
+                        nc.scalar.copy(out=res2[:], in_=back2[:])
+                        nc.sync.dma_start(out=out[h2 * P:(h2 + 1) * P, u0:u1], in_=res2[:])
+            else:
+                s1 = new("s1" + name, [P, t1 - t0], F32)
+                s2 = new("s2" + name, [P, t1 - t0], F32)
+                nc.vector.tensor_tensor(out=s1[:], in0=ys[h][:, t0:t1], in1=prods[0][:], op=ADD)
+                nc.vector.tensor_tensor(out=s2[:], in0=prods[1][:], in1=prods[2][:], op=ADD)
+                nc.vector.tensor_tensor(out=res[:], in0=s1[:], in1=s2[:], op=ADD)
+                nc.sync.dma_start(out=out[h * P:(h + 1) * P, t0:t1], in_=res[:])

@@ -24,12 +24,12 @@ PACK = 4
 HALVES = N // P
 GATHER_EXPERTS = 3
 RUN = 2
-LOADS = ["offs","xw","w0","w1","xs","w2","w3","w4","w5","w6","w7","b","w8","w9","w10","w11","pos0","pos1","w12","g00","g01","pos2","g02","gBl","gBr"]
+LOADS = ["offs","xw","w0","w1","xs","w2","w3","w4","w5","w6","w7","b","w8","w9","w10","w11","w12","pos0","pos1","g00","g01","pos2","g02","gBl","gBr"]
 SPLIT = []
-CASTS = ["S","S","S","S","S","S","S","VV","VV","VV","VV","VV","VV"]
+CASTS = ["S","S","S","S","S","S","S","V","VV","VV","VV","VV","VV"]
 TAGS = {}
 BANKS = []
-TERMS = ["s123","s123"]
+TERMS = ["s123","12s3"]
 PIECES = [["A",0,0,512,"pe"],["Bl",1,0,256,"pe"],["Br",1,256,512,"v"]]
 BIAS_COPIES = []
 
@@ -39,7 +39,7 @@ def tile_moe_shr_lin_silu_kernel(tc, x_words, x_scales, w, b, gate, offs, pos1, 
     with ExitStack() as ctx:
         keep = ctx.enter_context(tc.tile_pool(name="keep", bufs=1))
         psum = ctx.enter_context(tc.psum_pool(name="psum", bufs=1))
-        psum_mx = ctx.enter_context(tc.psum_pool(name="psum_mx", bufs=4))
+        psum_mx = ctx.enter_context(tc.psum_pool(name="psum_mx", bufs=6))
 
         def new(name, shape, dtype):
             return keep.tile(shape, dtype, name=name, tag=TAGS.get(name, name), align_bytes=64)
@@ -179,14 +179,14 @@ def tile_moe_shr_lin_silu_kernel(tc, x_words, x_scales, w, b, gate, offs, pos1, 
                 by_name = {"1": prods[0][:], "2": prods[1][:], "3": prods[2][:], "s": ys[h][:, t0:t1]}
                 terms = [by_name[c] for c in TERMS[on_tensor]]
                 blocks = [slice(j, j + P) for j in range(0, t1 - t0, P)]
-                turned = psum.tile([P, t1 - t0], F32, name="turned" + name, tag=turn_tags[on_tensor][0])
+                turned = (psum_mx if on_tensor else psum).tile([P, t1 - t0], F32, name="turned" + name, tag="acc" if on_tensor else "tu0")
                 for i, term in enumerate(terms):
                     for j, blk in enumerate(blocks):
                         nc.tensor.matmul(out=turned[:, blk], lhsT=term[:, blk], rhs=ident[:], is_transpose=True,
                                          start=(i == 0 and j == 0), stop=(i == len(terms) - 1 and j == len(blocks) - 1))
                 turned_sb = new("ts" + name, [P, t1 - t0], F32)
                 nc.scalar.copy(out=turned_sb[:], in_=turned[:])
-                back = psum.tile([P, t1 - t0], F32, name="back" + name, tag=turn_tags[on_tensor][1])
+                back = (psum_mx if on_tensor else psum).tile([P, t1 - t0], F32, name="back" + name, tag="acc" if on_tensor else "bk0")
                 waiting.append((back, turned_sb, blocks, res, h, t0, t1))
                 on_tensor += 1
                 if on_tensor == 2:
@@ -199,6 +199,9 @@ def tile_moe_shr_lin_silu_kernel(tc, x_words, x_scales, w, b, gate, offs, pos1, 
                 s1 = new("s1" + name, [P, t1 - t0], F32)
                 s2 = new("s2" + name, [P, t1 - t0], F32)
                 nc.vector.tensor_tensor(out=s1[:], in0=ys[h][:, t0:t1], in1=prods[0][:], op=ADD)
-                nc.vector.tensor_tensor(out=s2[:], in0=prods[1][:], in1=prods[2][:], op=ADD)
-                nc.vector.tensor_tensor(out=res[:], in0=s1[:], in1=s2[:], op=ADD)
+                blocks = [slice(j, j + P) for j in range(0, t1 - t0, P)]
+                for blk in blocks:
+                    nc.vector.tensor_tensor(out=s2[:, blk], in0=prods[1][:, blk], in1=prods[2][:, blk], op=ADD)
+                for blk in blocks:
+                    nc.vector.tensor_tensor(out=res[:, blk], in0=s1[:, blk], in1=s2[:, blk], op=ADD)
                 nc.sync.dma_start(out=out[h * P:(h + 1) * P, t0:t1], in_=res[:])

@@ -6,6 +6,7 @@ from concourse.masks import make_identity
 K, T, E, C, N = 512, 512, 12, 128, 256
 TOP = 3
 SLOTS = E * C
+SHARED = E
 FLOPS = 2 * K * N * (SLOTS + T)
 
 F32 = mybir.dt.float32
@@ -22,186 +23,179 @@ ADD = mybir.AluOpType.add
 P = 128
 PACK = 4
 HALVES = N // P
+LIST_COLUMN = 16
+SCALE_ROWS = 4
+BIAS_PITCH = 16
+ALIGN = 64
+
 GATHER_EXPERTS = 3
 RUN = 2
-LOADS = ["offs","xw","w0","w1","xs","w2","w3","w4","w5","w6","w7","b","w8","w9","w10","w11","w12","pos0","pos1","g00","g01","pos2","g02","gBl","gBr"]
-SPLIT = []
-CASTS = ["S","S","S","S","S","S","S","V","VV","VV","VV","VV","VV"]
-TAGS = {}
-BANKS = []
-TERMS = ["s123","12s3"]
-PIECES = [["A",0,0,512,"pe"],["Bl",1,0,256,"pe"],["Br",1,256,512,"v"]]
-BIAS_COPIES = []
+SCALAR_EXPERTS = 7
+SPLIT_EXPERT = E - 1
+MX_BANKS = 6
+TENSOR_TOKENS = 128
 
 
 def tile_moe_shr_lin_silu_kernel(tc, x_words, x_scales, w, b, gate, offs, pos1, pos2, pos3, out):
     nc = tc.nc
     with ExitStack() as ctx:
         keep = ctx.enter_context(tc.tile_pool(name="keep", bufs=1))
-        psum = ctx.enter_context(tc.psum_pool(name="psum", bufs=1))
-        psum_mx = ctx.enter_context(tc.psum_pool(name="psum_mx", bufs=6))
+        psum_sum = ctx.enter_context(tc.psum_pool(name="psum_sum", bufs=1))
+        psum_mx = ctx.enter_context(tc.psum_pool(name="psum_mx", bufs=MX_BANKS))
 
-        def new(name, shape, dtype):
-            return keep.tile(shape, dtype, name=name, tag=TAGS.get(name, name), align_bytes=64)
+        def sbuf(name, shape, dtype, tag=None):
+            return keep.tile(shape, dtype, name=name, tag=tag or name, align_bytes=ALIGN)
 
-        offs_sb = new("offs", [P, SLOTS // 16], U16)
-        pos_sb = [new("pos%d" % r, [P, T // 16], U16) for r in range(TOP)]
-        x_sb = new("xw", [P, T], I32)
-        xs_sb = new("xs", [P, T], U8)
-        b_sb = new("b", [P, HALVES, 16], F32)
-        gate_sb = {}
-        for name, h, t0, t1, how in PIECES:
-            if "g" + name in LOADS:
-                whole = new("g" + name, [P, TOP, t1 - t0], F32)
-                gate_sb[name] = [whole[:, r, :] for r in range(TOP)]
-                gate_sb["g" + name] = (whole, h, t0, t1)
-            else:
-                gate_sb[name] = [new("g%d%d" % (h, r), [P, T], F32)[:] for r in range(TOP)]
-        warm = new("warm", [P, 32], F32)
-        ident = new("ident", [P, P], F32)
-        raw = {}
-        for e in range(E + 1):
-            if e in SPLIT:
-                raw["%dA" % e] = new("raw%dA" % e, [P, PACK, P], F32)
-                raw["%dB" % e] = new("raw%dB" % e, [P, PACK, P], F32)
-            else:
-                raw["%d" % e] = new("raw%d" % e, [P, PACK, N], F32)
+        offs_sb = sbuf("offs", [P, SLOTS // LIST_COLUMN], U16)
+        pos_sb = [sbuf("pos%d" % r, [P, T // LIST_COLUMN], U16) for r in range(TOP)]
+        token_words = sbuf("token_words", [P, T], I32)
+        token_scales = sbuf("token_scales", [P, T], U8)
+        b_sb = sbuf("b", [P, HALVES, BIAS_PITCH], F32)
+        gate0 = [sbuf("gate0_%d" % r, [P, T], F32) for r in range(TOP)]
+        gate1_tensor = sbuf("gate1_tensor", [P, TOP, TENSOR_TOKENS], F32)
+        gate1_vector = sbuf("gate1_vector", [P, TOP, T - TENSOR_TOKENS], F32)
+        warm = sbuf("warm", [P, 32], F32)
+        ident = sbuf("ident", [P, P], F32)
+        raw = {e: sbuf("raw%d" % e, [P, PACK, N], F32) for e in range(SPLIT_EXPERT)}
+        raw_split = [sbuf("raw_split%d" % h, [P, PACK, P], F32) for h in range(HALVES)]
+        raw[SHARED] = sbuf("raw%d" % SHARED, [P, PACK, N], F32)
 
-        nc.gpsimd.memset(xs_sb[:].bitcast(I32), 0)
+        nc.gpsimd.memset(token_scales[:].bitcast(I32), 0)
         nc.gpsimd.memset(warm[:, 0:1], 0.0)
         nc.scalar.activation(out=warm[:, 16:17], in_=warm[:, 0:1], func=SILU)
 
-        for name in LOADS:
-            if name == "offs":
-                nc.sync.dma_start(offs_sb[:], offs)
-            elif name == "xw":
-                nc.sync.dma_start(out=x_sb[:], in_=x_words[0].rearrange("p t r -> p (t r)").bitcast(I32))
-            elif name == "xs":
-                for q in range(4):
-                    nc.sync.dma_start(out=xs_sb[32 * q:32 * q + 4, :].bitcast(I32), in_=x_scales[0, 4 * q:4 * q + 4, :].bitcast(I32))
-            elif name == "b":
-                nc.sync.dma_start(out=b_sb[:, :, 0:E + 1], in_=b.rearrange("(h p) e -> p h e", p=P))
-            elif name.startswith("pos"):
-                r = int(name[3])
-                nc.sync.dma_start(pos_sb[r][:], (pos1, pos2, pos3)[r])
-            elif name in gate_sb:
-                whole, h, t0, t1 = gate_sb[name]
-                nc.sync.dma_start(out=whole[:], in_=gate[:, h * P:(h + 1) * P, t0:t1].rearrange("r p t -> p r t"))
-            elif name.startswith("g"):
-                nc.sync.dma_start(out=gate_sb["A"][int(name[2])], in_=gate[int(name[2]), 0:P, :])
-            elif name[-1] in "AB":
-                h = "AB".index(name[-1])
-                nc.sync.dma_start(out=raw[name[1:]][:], in_=w[int(name[1:-1])].rearrange("(p j) n -> p j n", j=PACK)[:, :, h * P:(h + 1) * P])
-            else:
-                nc.sync.dma_start(out=raw[name[1:]][:], in_=w[int(name[1:])].rearrange("(p j) n -> p j n", j=PACK))
+        def rows_of(e):
+            return w[e].rearrange("(p j) n -> p j n", j=PACK)
 
-        bias = [b_sb[:, h, :] for h in range(HALVES)]
-        for h in BIAS_COPIES:
-            own = new("bias%d" % h, [P, 16], F32)
-            nc.gpsimd.tensor_copy(out=own[:, 0:E], in_=b_sb[:, h, 0:E])
-            bias[h] = own[:]
+        def load_weights(experts):
+            for e in experts:
+                nc.sync.dma_start(out=raw[e][:], in_=rows_of(e))
+
+        def load_split(h):
+            nc.sync.dma_start(out=raw_split[h][:], in_=rows_of(SPLIT_EXPERT)[:, :, h * P:(h + 1) * P])
+
+        def load_list_and_gate0(r):
+            nc.sync.dma_start(pos_sb[r][:], (pos1, pos2, pos3)[r])
+            nc.sync.dma_start(out=gate0[r][:], in_=gate[r, 0:P, :])
+
+        nc.sync.dma_start(offs_sb[:], offs)
+        nc.sync.dma_start(out=token_words[:], in_=x_words[0].rearrange("p t r -> p (t r)").bitcast(I32))
+        load_split(0)
+        load_weights(range(0, 2))
+        for q in range(P // 32):
+            rows = x_scales[0, SCALE_ROWS * q:SCALE_ROWS * (q + 1), :]
+            nc.sync.dma_start(out=token_scales[32 * q:32 * q + SCALE_ROWS, :].bitcast(I32), in_=rows.bitcast(I32))
+        load_weights(range(2, SCALAR_EXPERTS + 1))
+        nc.sync.dma_start(out=b_sb[:, :, 0:E + 1], in_=b.rearrange("(h p) e -> p h e", p=P))
+        load_weights(range(SCALAR_EXPERTS + 1, SPLIT_EXPERT))
+        load_weights([SHARED])
+        load_list_and_gate0(0)
+        load_split(1)
+        load_list_and_gate0(1)
+        load_list_and_gate0(2)
+        nc.sync.dma_start(out=gate1_tensor[:], in_=gate[:, P:N, 0:TENSOR_TOKENS].rearrange("r p t -> p r t"))
+        nc.sync.dma_start(out=gate1_vector[:], in_=gate[:, P:N, TENSOR_TOKENS:T].rearrange("r p t -> p r t"))
+
+        bias_shared = sbuf("bias_shared", [P, HALVES], F32, tag="raw_split1")
+        nc.scalar.copy(out=bias_shared[:], in_=b_sb[:, :, SHARED])
         make_identity(nc, ident[:])
 
-        y = [new("y%d" % h, [P, SLOTS], F32) for h in range(HALVES)]
-        ys = [new("ys%d" % h, [P, T], F32) for h in range(HALVES)]
-        width = GATHER_EXPERTS * C
-        xg, xsg, banks = {}, {}, {}
+        y = [sbuf("y%d" % h, [P, SLOTS], F32) for h in range(HALVES)]
+        ys = [sbuf("ys%d" % h, [P, T], F32) for h in range(HALVES)]
 
         def gather_tokens(g):
-            xg[g] = new("xg%d" % g, [P, width], U32)
-            xsg[g] = new("xsg%d" % g, [P, width], U8)
-            lst = offs_sb[:, g * width // 16:(g + 1) * width // 16]
-            nc.vector.tensor_copy(out=xg[g][:], in_=x_sb[:].bitcast(U32).indirect(lst))
-            nc.vector.tensor_copy(out=xsg[g][:], in_=xs_sb[:].indirect(lst))
+            width = GATHER_EXPERTS * C
+            words = sbuf("slot_words%d" % g, [P, width], U32)
+            scales = sbuf("slot_scales%d" % g, [P, width], U8)
+            entries = offs_sb[:, g * width // LIST_COLUMN:(g + 1) * width // LIST_COLUMN]
+            nc.vector.tensor_copy(out=words[:], in_=token_words[:].bitcast(U32).indirect(entries))
+            nc.vector.tensor_copy(out=scales[:], in_=token_scales[:].indirect(entries))
+            return words, scales
 
-        def expert(e):
-            pieces = CASTS[e]
-            cols = N // len(pieces)
-            operands = []
-            for j, engine in enumerate(pieces):
-                sfx = "" if len(pieces) == 1 else "AB"[j]
-                codes = new("codes%d%s" % (e, sfx), [P, cols], U32)
-                scales = new("scales%d%s" % (e, sfx), [P, cols], U8)
-                grouped = new("grouped%d%s" % (e, sfx), [P, cols, PACK], BF16)
-                src = raw["%d%s" % (e, sfx)][:] if e in SPLIT else raw["%d" % e][:, :, j * cols:(j + 1) * cols]
-                copy = nc.vector.tensor_copy if engine == "V" else nc.scalar.copy
-                copy(out=grouped[:].rearrange("p (c i) t -> p c t i", i=RUN),
-                     in_=src.rearrange("p t (c i) -> p c t i", i=RUN))
-                nc.vector.quantize_mx(out=codes[:].bitcast(FP8X4), scales=scales[:],
-                                      in_=grouped[:].rearrange("p n t -> p (n t)"))
-                for c0 in range(0, cols, P):
-                    operands.append((codes[:, c0:c0 + P], scales[:, c0:c0 + P]))
+        def quantise(name, copy, rows):
+            width = rows.shape[2]
+            codes = sbuf("codes" + name, [P, width], U32)
+            scales = sbuf("scales" + name, [P, width], U8)
+            grouped = sbuf("grouped" + name, [P, width, PACK], BF16)
+            copy(out=grouped[:].rearrange("p (c i) j -> p c j i", i=RUN), in_=rows.rearrange("p j (c i) -> p c j i", i=RUN))
+            nc.vector.quantize_mx(out=codes[:].bitcast(FP8X4), scales=scales[:], in_=grouped[:].rearrange("p n j -> p (n j)"))
+            return [(codes[:, c:c + P], scales[:, c:c + P]) for c in range(0, width, P)]
 
-            for h in range(HALVES):
-                if e < E:
-                    g, c0 = divmod(e, GATHER_EXPERTS)
-                    slots = slice(c0 * C, (c0 + 1) * C)
-                    words, word_scales, dst = xg[g][:, slots], xsg[g][:, slots], y[h][:, e * C:(e + 1) * C]
-                else:
-                    words, word_scales, dst = x_sb[:], xs_sb[:], ys[h][:]
-                banked = h == 1 and e < E and len(BANKS) > 0
-                if banked:
-                    k = [i for i in range(len(BANKS)) if e in BANKS[i]][0]
-                    if k not in banks:
-                        banks[k] = psum.tile([P, 4 * C], F32, name="bank%d" % k)
-                    place = BANKS[k].index(e)
-                    acc = banks[k][:, place * C:(place + 1) * C]
-                else:
-                    acc_tile = psum_mx.tile([P, words.shape[1]], F32, name="acc")
-                    acc = acc_tile[:]
-                nc.tensor.matmul_mx(out=acc, lhsT=operands[h][0].bitcast(FP8X4), lhsT_scale=operands[h][1],
-                                    rhs=words.bitcast(FP8X4), rhs_scale=word_scales, start=True, stop=True)
-                if not banked:
-                    nc.scalar.activation(out=dst, in_=acc, func=SILU, bias=(bias[h] if e < E else b_sb[:, h, :])[:, e:e + 1])
-                elif e == E - 1:
-                    for k in range(len(BANKS)):
-                        for place, e2 in enumerate(BANKS[k]):
-                            nc.scalar.activation(out=y[1][:, e2 * C:(e2 + 1) * C], in_=banks[k][:, place * C:(place + 1) * C],
-                                                 func=SILU, bias=bias[1][:, e2:e2 + 1])
+        def quantise_expert(e):
+            if e == SPLIT_EXPERT:
+                return [quantise("%d_%d" % (e, h), nc.scalar.copy, raw_split[h][:])[0] for h in range(HALVES)]
+            if e < SCALAR_EXPERTS:
+                return quantise("%d" % e, nc.scalar.copy, raw[e][:])
+            if e == SCALAR_EXPERTS:
+                return quantise("%d" % e, nc.vector.tensor_copy, raw[e][:])
+            return [quantise("%d_%d" % (e, h), nc.vector.tensor_copy, raw[e][:, :, h * P:(h + 1) * P])[0] for h in range(HALVES)]
 
-        for e in range(E + 1):
-            if e < E and e % GATHER_EXPERTS == 0:
-                gather_tokens(e // GATHER_EXPERTS)
-            expert(e)
+        def multiply(operand, words, scales, result, bias):
+            acc = psum_mx.tile([P, words.shape[1]], F32, name="acc")
+            nc.tensor.matmul_mx(out=acc[:], lhsT=operand[0].bitcast(FP8X4), lhsT_scale=operand[1],
+                                rhs=words.bitcast(FP8X4), rhs_scale=scales, start=True, stop=True)
+            nc.scalar.activation(out=result, in_=acc[:], func=SILU, bias=bias)
 
-        turn_tags = [("tu0", "bk0"), ("bank0", "bank1") if BANKS else ("tu1", "bk1")]
-        on_tensor = 0
-        waiting = []
-        for name, h, t0, t1, how in PIECES:
-            prods = []
+        for g in range(E // GATHER_EXPERTS):
+            slot_words, slot_scales = gather_tokens(g)
+            for place in range(GATHER_EXPERTS):
+                e = g * GATHER_EXPERTS + place
+                cols = slice(place * C, (place + 1) * C)
+                for h, operand in enumerate(quantise_expert(e)):
+                    multiply(operand, slot_words[:, cols], slot_scales[:, cols], y[h][:, e * C:(e + 1) * C], b_sb[:, h, e:e + 1])
+        for h, operand in enumerate(quantise_expert(SHARED)):
+            multiply(operand, token_words[:], token_scales[:], ys[h][:], bias_shared[:, h:h + 1])
+
+        def products(name, h, t0, t1, gates):
+            tiles = []
             for r in range(TOP):
-                prod = new("%s%d" % (name, r + 1), [P, t1 - t0], F32)
-                nc.vector.tensor_tensor(out=prod[:], in0=y[h][:].indirect(pos_sb[r][:, t0 // 16:t1 // 16]),
-                                        in1=gate_sb[name][r], op=MULT)
-                prods.append(prod)
-            res = new("res" + name, [P, t1 - t0], F32)
-            if how == "pe":
-                by_name = {"1": prods[0][:], "2": prods[1][:], "3": prods[2][:], "s": ys[h][:, t0:t1]}
-                terms = [by_name[c] for c in TERMS[on_tensor]]
-                blocks = [slice(j, j + P) for j in range(0, t1 - t0, P)]
-                turned = (psum_mx if on_tensor else psum).tile([P, t1 - t0], F32, name="turned" + name, tag="acc" if on_tensor else "tu0")
-                for i, term in enumerate(terms):
-                    for j, blk in enumerate(blocks):
-                        nc.tensor.matmul(out=turned[:, blk], lhsT=term[:, blk], rhs=ident[:], is_transpose=True,
-                                         start=(i == 0 and j == 0), stop=(i == len(terms) - 1 and j == len(blocks) - 1))
-                turned_sb = new("ts" + name, [P, t1 - t0], F32)
-                nc.scalar.copy(out=turned_sb[:], in_=turned[:])
-                back = (psum_mx if on_tensor else psum).tile([P, t1 - t0], F32, name="back" + name, tag="acc" if on_tensor else "bk0")
-                waiting.append((back, turned_sb, blocks, res, h, t0, t1))
-                on_tensor += 1
-                if on_tensor == 2:
-                    for back2, turned2, blocks2, res2, h2, u0, u1 in waiting:
-                        for blk in blocks2:
-                            nc.tensor.transpose(back2[:, blk], turned2[:, blk], ident[:])
-                        nc.scalar.copy(out=res2[:], in_=back2[:])
-                        nc.sync.dma_start(out=out[h2 * P:(h2 + 1) * P, u0:u1], in_=res2[:])
-            else:
-                s1 = new("s1" + name, [P, t1 - t0], F32)
-                s2 = new("s2" + name, [P, t1 - t0], F32)
-                nc.vector.tensor_tensor(out=s1[:], in0=ys[h][:, t0:t1], in1=prods[0][:], op=ADD)
-                blocks = [slice(j, j + P) for j in range(0, t1 - t0, P)]
-                for blk in blocks:
-                    nc.vector.tensor_tensor(out=s2[:, blk], in0=prods[1][:, blk], in1=prods[2][:, blk], op=ADD)
-                for blk in blocks:
-                    nc.vector.tensor_tensor(out=res[:, blk], in0=s1[:, blk], in1=s2[:, blk], op=ADD)
-                nc.sync.dma_start(out=out[h * P:(h + 1) * P, t0:t1], in_=res[:])
+                product = sbuf("%s%d" % (name, r), [P, t1 - t0], F32)
+                entries = pos_sb[r][:, t0 // LIST_COLUMN:t1 // LIST_COLUMN]
+                nc.vector.tensor_tensor(out=product[:], in0=y[h][:].indirect(entries), in1=gates[r], op=MULT)
+                tiles.append(product[:])
+            return tiles
+
+        def blocks_of(width):
+            return [slice(c, c + P) for c in range(0, width, P)]
+
+        def add_turned(name, terms, turned):
+            passes = [(term, block) for term in terms for block in blocks_of(terms[0].shape[1])]
+            for i, (term, block) in enumerate(passes):
+                nc.tensor.matmul(out=turned[:, block], lhsT=term[:, block], rhs=ident[:], is_transpose=True,
+                                 start=(i == 0), stop=(i == len(passes) - 1))
+            turned_sb = sbuf(name, [P, terms[0].shape[1]], F32)
+            nc.scalar.copy(out=turned_sb[:], in_=turned[:])
+            return turned_sb
+
+        def turn_back_and_store(name, turned_sb, back, dst):
+            width = dst.shape[1]
+            for block in blocks_of(width):
+                nc.tensor.transpose(back[:, block], turned_sb[:, block], ident[:])
+            result = sbuf(name, [P, width], F32)
+            nc.scalar.copy(out=result[:], in_=back[:])
+            nc.sync.dma_start(out=dst, in_=result[:])
+
+        p0 = products("product0_", 0, 0, T, [tile_r[:] for tile_r in gate0])
+        turned0 = psum_sum.tile([P, T], F32, name="turned0")
+        turned0_sb = add_turned("turned0_sb", [p0[0], ys[0][:], p0[1], p0[2]], turned0)
+        back0 = psum_sum.tile([P, T], F32, name="back0")
+
+        p1 = products("product1_tensor", 1, 0, TENSOR_TOKENS, [gate1_tensor[:, r, :] for r in range(TOP)])
+        turned1 = psum_mx.tile([P, TENSOR_TOKENS], F32, name="turned1", tag="acc")
+        turned1_sb = add_turned("turned1_sb", [p1[0], p1[1], ys[1][:, 0:TENSOR_TOKENS], p1[2]], turned1)
+        back1 = psum_mx.tile([P, TENSOR_TOKENS], F32, name="back1", tag="acc")
+
+        turn_back_and_store("result0", turned0_sb, back0, out[0:P, :])
+        turn_back_and_store("result1_tensor", turned1_sb, back1, out[P:N, 0:TENSOR_TOKENS])
+
+        rest = T - TENSOR_TOKENS
+        p2 = products("product1_vector", 1, TENSOR_TOKENS, T, [gate1_vector[:, r, :] for r in range(TOP)])
+        result = sbuf("result1_vector", [P, rest], F32)
+        pair_a = sbuf("pair_a", [P, rest], F32)
+        pair_b = sbuf("pair_b", [P, rest], F32)
+        nc.vector.tensor_tensor(out=pair_a[:], in0=ys[1][:, TENSOR_TOKENS:T], in1=p2[0], op=ADD)
+        for block in blocks_of(rest):
+            nc.vector.tensor_tensor(out=pair_b[:, block], in0=p2[1][:, block], in1=p2[2][:, block], op=ADD)
+        for block in blocks_of(rest):
+            nc.vector.tensor_tensor(out=result[:, block], in0=pair_a[:, block], in1=pair_b[:, block], op=ADD)
+        nc.sync.dma_start(out=out[P:N, TENSOR_TOKENS:T], in_=result[:])

@@ -31,7 +31,6 @@ ALIGN = 64
 GATHER_EXPERTS = 3
 RUN = 2
 SCALAR_EXPERTS = 7
-SPLIT_EXPERT = E - 1
 MX_BANKS = 6
 TENSOR_TOKENS = 128
 
@@ -43,8 +42,8 @@ def tile_moe_shr_lin_silu_kernel(tc, x_words, x_scales, w, b, gate, offs, pos1, 
         psum_sum = ctx.enter_context(tc.psum_pool(name="psum_sum", bufs=1))
         psum_mx = ctx.enter_context(tc.psum_pool(name="psum_mx", bufs=MX_BANKS))
 
-        def sbuf(name, shape, dtype, tag=None):
-            return keep.tile(shape, dtype, name=name, tag=tag or name, align_bytes=ALIGN)
+        def sbuf(name, shape, dtype):
+            return keep.tile(shape, dtype, name=name, align_bytes=ALIGN)
 
         offs_sb = sbuf("offs", [P, SLOTS // LIST_COLUMN], U16)
         pos_sb = [sbuf("pos%d" % r, [P, T // LIST_COLUMN], U16) for r in range(TOP)]
@@ -54,25 +53,14 @@ def tile_moe_shr_lin_silu_kernel(tc, x_words, x_scales, w, b, gate, offs, pos1, 
         gate0 = [sbuf("gate0_%d" % r, [P, T], F32) for r in range(TOP)]
         gate1_tensor = sbuf("gate1_tensor", [P, TOP, TENSOR_TOKENS], F32)
         gate1_vector = sbuf("gate1_vector", [P, TOP, T - TENSOR_TOKENS], F32)
-        warm = sbuf("warm", [P, 32], F32)
         ident = sbuf("ident", [P, P], F32)
-        raw = {e: sbuf("raw%d" % e, [P, PACK, N], F32) for e in range(SPLIT_EXPERT)}
-        raw_split = [sbuf("raw_split%d" % h, [P, PACK, P], F32) for h in range(HALVES)]
-        raw[SHARED] = sbuf("raw%d" % SHARED, [P, PACK, N], F32)
+        raw = [sbuf("raw%d" % e, [P, PACK, N], F32) for e in range(E + 1)]
 
         nc.gpsimd.memset(token_scales[:].bitcast(I32), 0)
-        nc.gpsimd.memset(warm[:, 0:1], 0.0)
-        nc.scalar.activation(out=warm[:, 16:17], in_=warm[:, 0:1], func=SILU)
-
-        def rows_of(e):
-            return w[e].rearrange("(p j) n -> p j n", j=PACK)
 
         def load_weights(experts):
             for e in experts:
-                nc.sync.dma_start(out=raw[e][:], in_=rows_of(e))
-
-        def load_split(h):
-            nc.sync.dma_start(out=raw_split[h][:], in_=rows_of(SPLIT_EXPERT)[:, :, h * P:(h + 1) * P])
+                nc.sync.dma_start(out=raw[e][:], in_=w[e].rearrange("(p j) n -> p j n", j=PACK))
 
         def load_list_and_gate0(r):
             nc.sync.dma_start(pos_sb[r][:], (pos1, pos2, pos3)[r])
@@ -80,24 +68,18 @@ def tile_moe_shr_lin_silu_kernel(tc, x_words, x_scales, w, b, gate, offs, pos1, 
 
         nc.sync.dma_start(offs_sb[:], offs)
         nc.sync.dma_start(out=token_words[:], in_=x_words[0].rearrange("p t r -> p (t r)").bitcast(I32))
-        load_split(0)
         load_weights(range(0, 2))
         for q in range(P // 32):
             rows = x_scales[0, SCALE_ROWS * q:SCALE_ROWS * (q + 1), :]
             nc.sync.dma_start(out=token_scales[32 * q:32 * q + SCALE_ROWS, :].bitcast(I32), in_=rows.bitcast(I32))
         load_weights(range(2, SCALAR_EXPERTS + 1))
         nc.sync.dma_start(out=b_sb[:, :, 0:E + 1], in_=b.rearrange("(h p) e -> p h e", p=P))
-        load_weights(range(SCALAR_EXPERTS + 1, SPLIT_EXPERT))
-        load_weights([SHARED])
-        load_list_and_gate0(0)
-        load_split(1)
-        load_list_and_gate0(1)
-        load_list_and_gate0(2)
+        load_weights(range(SCALAR_EXPERTS + 1, E + 1))
+        for r in range(TOP):
+            load_list_and_gate0(r)
         nc.sync.dma_start(out=gate1_tensor[:], in_=gate[:, P:N, 0:TENSOR_TOKENS].rearrange("r p t -> p r t"))
         nc.sync.dma_start(out=gate1_vector[:], in_=gate[:, P:N, TENSOR_TOKENS:T].rearrange("r p t -> p r t"))
 
-        bias_shared = sbuf("bias_shared", [P, HALVES], F32, tag="raw_split1")
-        nc.scalar.copy(out=bias_shared[:], in_=b_sb[:, :, SHARED])
         make_identity(nc, ident[:])
 
         y = [sbuf("y%d" % h, [P, SLOTS], F32) for h in range(HALVES)]
@@ -122,8 +104,6 @@ def tile_moe_shr_lin_silu_kernel(tc, x_words, x_scales, w, b, gate, offs, pos1, 
             return [(codes[:, c:c + P], scales[:, c:c + P]) for c in range(0, width, P)]
 
         def quantise_expert(e):
-            if e == SPLIT_EXPERT:
-                return [quantise("%d_%d" % (e, h), nc.scalar.copy, raw_split[h][:])[0] for h in range(HALVES)]
             if e < SCALAR_EXPERTS:
                 return quantise("%d" % e, nc.scalar.copy, raw[e][:])
             if e == SCALAR_EXPERTS:
@@ -144,7 +124,7 @@ def tile_moe_shr_lin_silu_kernel(tc, x_words, x_scales, w, b, gate, offs, pos1, 
                 for h, operand in enumerate(quantise_expert(e)):
                     multiply(operand, slot_words[:, cols], slot_scales[:, cols], y[h][:, e * C:(e + 1) * C], b_sb[:, h, e:e + 1])
         for h, operand in enumerate(quantise_expert(SHARED)):
-            multiply(operand, token_words[:], token_scales[:], ys[h][:], bias_shared[:, h:h + 1])
+            multiply(operand, token_words[:], token_scales[:], ys[h][:], b_sb[:, h, SHARED:SHARED + 1])
 
         def products(name, h, t0, t1, gates):
             tiles = []

from contextlib import ExitStack

import concourse.mybir as mybir
from concourse.masks import make_identity

K, T, E, C, N = 512, 512, 12, 128, 256
TOP = 3
SLOTS = E * C
SHARED = E
FLOPS = 2 * K * N * (SLOTS + T)

F32 = mybir.dt.float32
BF16 = mybir.dt.bfloat16
I32 = mybir.dt.int32
U32 = mybir.dt.uint32
U16 = mybir.dt.uint16
U8 = mybir.dt.uint8
FP8X4 = mybir.dt.float8_e4m3fn_x4
SILU = mybir.ActivationFunctionType.Silu
MULT = mybir.AluOpType.mult
ADD = mybir.AluOpType.add

P = 128
PACK = 4
HALVES = N // P
LIST_COLUMN = 16
SCALE_ROWS = 4
BIAS_PITCH = 16
ALIGN = 64

GATHER_EXPERTS = 3
RUN = 2
SCALAR_EXPERTS = 7
MX_BANKS = 6
TENSOR_TOKENS = 128


def tile_moe_shr_lin_silu_kernel(tc, x_words, x_scales, w, b, gate, offs, pos1, pos2, pos3, out):
    nc = tc.nc
    with ExitStack() as ctx:
        keep = ctx.enter_context(tc.tile_pool(name="keep", bufs=1))
        psum_sum = ctx.enter_context(tc.psum_pool(name="psum_sum", bufs=1))
        psum_mx = ctx.enter_context(tc.psum_pool(name="psum_mx", bufs=MX_BANKS))

        def sbuf(name, shape, dtype):
            return keep.tile(shape, dtype, name=name, align_bytes=ALIGN)

        offs_sb = sbuf("offs", [P, SLOTS // LIST_COLUMN], U16)
        pos_sb = [sbuf("pos%d" % r, [P, T // LIST_COLUMN], U16) for r in range(TOP)]
        token_words = sbuf("token_words", [P, T], I32)
        token_scales = sbuf("token_scales", [P, T], U8)
        b_sb = sbuf("b", [P, HALVES, BIAS_PITCH], F32)
        gate0 = [sbuf("gate0_%d" % r, [P, T], F32) for r in range(TOP)]
        gate1_tensor = sbuf("gate1_tensor", [P, TOP, TENSOR_TOKENS], F32)
        gate1_vector = sbuf("gate1_vector", [P, TOP, T - TENSOR_TOKENS], F32)
        ident = sbuf("ident", [P, P], F32)
        raw = [sbuf("raw%d" % e, [P, PACK, N], F32) for e in range(E + 1)]

        nc.gpsimd.memset(token_scales[:].bitcast(I32), 0)

        def load_weights(experts):
            for e in experts:
                nc.sync.dma_start(out=raw[e][:], in_=w[e].rearrange("(p j) n -> p j n", j=PACK))

        def load_list_and_gate0(r):
            nc.sync.dma_start(pos_sb[r][:], (pos1, pos2, pos3)[r])
            nc.sync.dma_start(out=gate0[r][:], in_=gate[r, 0:P, :])

        nc.sync.dma_start(offs_sb[:], offs)
        nc.sync.dma_start(out=token_words[:], in_=x_words[0].rearrange("p t r -> p (t r)").bitcast(I32))
        load_weights(range(0, 2))
        for q in range(P // 32):
            rows = x_scales[0, SCALE_ROWS * q:SCALE_ROWS * (q + 1), :]
            nc.sync.dma_start(out=token_scales[32 * q:32 * q + SCALE_ROWS, :].bitcast(I32), in_=rows.bitcast(I32))
        load_weights(range(2, SCALAR_EXPERTS + 1))
        nc.sync.dma_start(out=b_sb[:, :, 0:E + 1], in_=b.rearrange("(h p) e -> p h e", p=P))
        load_weights(range(SCALAR_EXPERTS + 1, E + 1))
        for r in range(TOP):
            load_list_and_gate0(r)
        nc.sync.dma_start(out=gate1_tensor[:], in_=gate[:, P:N, 0:TENSOR_TOKENS].rearrange("r p t -> p r t"))
        nc.sync.dma_start(out=gate1_vector[:], in_=gate[:, P:N, TENSOR_TOKENS:T].rearrange("r p t -> p r t"))

        make_identity(nc, ident[:])

        y = [sbuf("y%d" % h, [P, SLOTS], F32) for h in range(HALVES)]
        ys = [sbuf("ys%d" % h, [P, T], F32) for h in range(HALVES)]

        def gather_tokens(g):
            width = GATHER_EXPERTS * C
            words = sbuf("slot_words%d" % g, [P, width], U32)
            scales = sbuf("slot_scales%d" % g, [P, width], U8)
            entries = offs_sb[:, g * width // LIST_COLUMN:(g + 1) * width // LIST_COLUMN]
            nc.vector.tensor_copy(out=words[:], in_=token_words[:].bitcast(U32).indirect(entries))
            nc.vector.tensor_copy(out=scales[:], in_=token_scales[:].indirect(entries))
            return words, scales

        def quantise(name, copy, rows):
            width = rows.shape[2]
            codes = sbuf("codes" + name, [P, width], U32)
            scales = sbuf("scales" + name, [P, width], U8)
            grouped = sbuf("grouped" + name, [P, width, PACK], BF16)
            copy(out=grouped[:].rearrange("p (c i) j -> p c j i", i=RUN), in_=rows.rearrange("p j (c i) -> p c j i", i=RUN))
            nc.vector.quantize_mx(out=codes[:].bitcast(FP8X4), scales=scales[:], in_=grouped[:].rearrange("p n j -> p (n j)"))
            return [(codes[:, c:c + P], scales[:, c:c + P]) for c in range(0, width, P)]

        def quantise_expert(e):
            if e < SCALAR_EXPERTS:
                return quantise("%d" % e, nc.scalar.copy, raw[e][:])
            if e == SCALAR_EXPERTS:
                return quantise("%d" % e, nc.vector.tensor_copy, raw[e][:])
            return [quantise("%d_%d" % (e, h), nc.vector.tensor_copy, raw[e][:, :, h * P:(h + 1) * P])[0] for h in range(HALVES)]

        def multiply(operand, words, scales, result, bias):
            acc = psum_mx.tile([P, words.shape[1]], F32, name="acc")
            nc.tensor.matmul_mx(out=acc[:], lhsT=operand[0].bitcast(FP8X4), lhsT_scale=operand[1],
                                rhs=words.bitcast(FP8X4), rhs_scale=scales, start=True, stop=True)
            nc.scalar.activation(out=result, in_=acc[:], func=SILU, bias=bias)

        for g in range(E // GATHER_EXPERTS):
            slot_words, slot_scales = gather_tokens(g)
            for place in range(GATHER_EXPERTS):
                e = g * GATHER_EXPERTS + place
                cols = slice(place * C, (place + 1) * C)
                for h, operand in enumerate(quantise_expert(e)):
                    multiply(operand, slot_words[:, cols], slot_scales[:, cols], y[h][:, e * C:(e + 1) * C], b_sb[:, h, e:e + 1])
        for h, operand in enumerate(quantise_expert(SHARED)):
            multiply(operand, token_words[:], token_scales[:], ys[h][:], b_sb[:, h, SHARED:SHARED + 1])

        def products(name, h, t0, t1, gates):
            tiles = []
            for r in range(TOP):
                product = sbuf("%s%d" % (name, r), [P, t1 - t0], F32)
                entries = pos_sb[r][:, t0 // LIST_COLUMN:t1 // LIST_COLUMN]
                nc.vector.tensor_tensor(out=product[:], in0=y[h][:].indirect(entries), in1=gates[r], op=MULT)
                tiles.append(product[:])
            return tiles

        def blocks_of(width):
            return [slice(c, c + P) for c in range(0, width, P)]

        def add_turned(name, terms, turned):
            passes = [(term, block) for term in terms for block in blocks_of(terms[0].shape[1])]
            for i, (term, block) in enumerate(passes):
                nc.tensor.matmul(out=turned[:, block], lhsT=term[:, block], rhs=ident[:], is_transpose=True,
                                 start=(i == 0), stop=(i == len(passes) - 1))
            turned_sb = sbuf(name, [P, terms[0].shape[1]], F32)
            nc.scalar.copy(out=turned_sb[:], in_=turned[:])
            return turned_sb

        def turn_back_and_store(name, turned_sb, back, dst):
            width = dst.shape[1]
            for block in blocks_of(width):
                nc.tensor.transpose(back[:, block], turned_sb[:, block], ident[:])
            result = sbuf(name, [P, width], F32)
            nc.scalar.copy(out=result[:], in_=back[:])
            nc.sync.dma_start(out=dst, in_=result[:])

        p0 = products("product0_", 0, 0, T, [tile_r[:] for tile_r in gate0])
        turned0 = psum_sum.tile([P, T], F32, name="turned0")
        turned0_sb = add_turned("turned0_sb", [p0[0], ys[0][:], p0[1], p0[2]], turned0)
        back0 = psum_sum.tile([P, T], F32, name="back0")

        p1 = products("product1_tensor", 1, 0, TENSOR_TOKENS, [gate1_tensor[:, r, :] for r in range(TOP)])
        turned1 = psum_mx.tile([P, TENSOR_TOKENS], F32, name="turned1", tag="acc")
        turned1_sb = add_turned("turned1_sb", [p1[0], p1[1], ys[1][:, 0:TENSOR_TOKENS], p1[2]], turned1)
        back1 = psum_mx.tile([P, TENSOR_TOKENS], F32, name="back1", tag="acc")

        turn_back_and_store("result0", turned0_sb, back0, out[0:P, :])
        turn_back_and_store("result1_tensor", turned1_sb, back1, out[P:N, 0:TENSOR_TOKENS])

        rest = T - TENSOR_TOKENS
        p2 = products("product1_vector", 1, TENSOR_TOKENS, T, [gate1_vector[:, r, :] for r in range(TOP)])
        result = sbuf("result1_vector", [P, rest], F32)
        pair_a = sbuf("pair_a", [P, rest], F32)
        pair_b = sbuf("pair_b", [P, rest], F32)
        nc.vector.tensor_tensor(out=pair_a[:], in0=ys[1][:, TENSOR_TOKENS:T], in1=p2[0], op=ADD)
        for block in blocks_of(rest):
            nc.vector.tensor_tensor(out=pair_b[:, block], in0=p2[1][:, block], in1=p2[2][:, block], op=ADD)
        for block in blocks_of(rest):
            nc.vector.tensor_tensor(out=result[:, block], in0=pair_a[:, block], in1=pair_b[:, block], op=ADD)
        nc.sync.dma_start(out=out[P:N, TENSOR_TOKENS:T], in_=result[:])
